import numpy as np
import ml_dtypes


def mxq(x, axis, fmt="e4m3"):
    dtype, down = {"e4m3": (ml_dtypes.float8_e4m3fn, 7), "e5m2": (ml_dtypes.float8_e5m2, 14)}[fmt]
    v = np.moveaxis(np.asarray(x, np.float32).astype(ml_dtypes.bfloat16).astype(np.float64), axis, -1)
    blocks = v.reshape(v.shape[:-1] + (-1, 32))
    amax = np.abs(blocks).max(-1, keepdims=True)
    byte = np.maximum(np.where(amax > 0, np.frexp(amax)[1] - 1 + 127, 0) - down, 1)
    scale = np.exp2(byte - 127.0)
    codes = (blocks / scale).astype(np.float32).astype(dtype).astype(np.float64)
    return np.moveaxis((codes * scale).reshape(v.shape), -1, axis)


WIDE = False


def mx_kscale(k):
    if not WIDE:
        return np.ones(k)
    levels = np.array([10, -10, 5, -5, 0])
    if k % 512:
        return np.exp2(np.random.permutation(np.resize(levels, k // 32))).repeat(32)
    a = np.empty((k // 512, 16))
    for p in range(k // 512):
        a[p, :8] = np.random.permutation(np.resize(levels, 8))
        for g in range(8):
            far = levels[np.abs(levels - a[p, g]) >= 10]
            a[p, g + 8] = far[np.random.randint(len(far))]
    return np.exp2(a.ravel()).repeat(32)


def f64(x):
    return np.asarray(x).astype(np.float64)


def striped(idx):
    return np.tile(idx.reshape(-1, 16).T, (8, 1)).astype(np.uint16)


def unstriped(offs):
    return offs[:16].T.reshape(-1).astype(np.int64)


E2M1 = np.array([0.0, 0.5, 1.0, 1.5, 2.0, 3.0, 4.0, 6.0, -0.0, -0.5, -1.0, -1.5, -2.0, -3.0, -4.0, -6.0])


def pack_weight(w, fmt):
    k, n = w.shape
    w = f64(np.asarray(w, np.float32).astype(ml_dtypes.bfloat16)).reshape(k // 32, 32, n)
    amax = np.abs(w).max(1)
    if fmt == "e4m3":
        byte = np.frexp(amax)[1] - 1 + 127 - 7
    else:
        mant, ex = np.frexp(amax / 6.0)
        byte = np.where(mant > 0.5, ex, ex - 1) + 127
    byte = np.clip(np.where(amax > 0, byte, 1), 1, 254)
    scaled = (w * np.exp2(127.0 - byte)[:, None, :]).reshape(k, n).astype(np.float32)
    by_word = np.ascontiguousarray(scaled.reshape(k // 512, 128, 4, n).transpose(0, 1, 3, 2))
    if fmt == "e4m3":
        words = by_word.astype(ml_dtypes.float8_e4m3fn).view(np.uint8)
    else:
        c = by_word.astype(ml_dtypes.float4_e2m1fn).view(np.uint8) & 0xF
        words = (c[..., 0::2] | (c[..., 1::2] << 4)).reshape(k // 512, 128, 2 * n)
    return np.ascontiguousarray(words), np.ascontiguousarray(byte.astype(np.uint8).reshape(k // 512, 16, n))


def unpack_weight(words, scales, fmt):
    g, _, n = scales.shape
    words = np.ascontiguousarray(words).reshape(g, 128, n, -1)
    if fmt == "e4m3":
        vals = words.view(ml_dtypes.float8_e4m3fn).astype(np.float64)
    else:
        nib = np.empty((g, 128, n, 4), np.uint8)
        nib[..., 0::2] = words & 0xF
        nib[..., 1::2] = words >> 4
        vals = E2M1[nib]
    vals = vals * np.repeat(np.exp2(scales.astype(np.float64) - 127.0), 8, axis=1)[..., None]
    return vals.transpose(0, 1, 3, 2).reshape(g * 512, n)


def gelu(v):
    return 0.5 * v * (1.0 + np.tanh(np.sqrt(2.0 / np.pi) * (v + 0.044715 * v**3)))


K, H, N, T, S, P, P2 = 1024, 512, 512, 4096, 2048, 1024, 512


def setup_inputs():
    n = np.random.standard_normal
    s = mx_kscale(K)[:, None]
    u = mx_kscale(H)[:, None]
    tab_words, tab_scales = pack_weight(n((K, T)) * s, "e4m3")
    w2_words, w2_scales = pack_weight(1.5 * n((K, H)) / np.sqrt(K) / s, "e2m1")
    w3_words, w3_scales = pack_weight(n((H, N)) / np.sqrt(H) / u, "e4m3")
    return {
        "tab_words": tab_words, "tab_scales": tab_scales,
        "offs": striped(np.random.permutation(T)[:S]),
        "pos1": striped(np.random.permutation(S)[:P]),
        "pos2": striped(np.random.permutation(S)[:P]),
        "pos3": striped(np.random.permutation(P)[:P2]),
        "pos4": striped(np.random.permutation(S)[:P2]),
        "w1": (1.5 * n((K, H)) / np.sqrt(K) / s * u.T).astype(np.float32),
        "w2_words": w2_words, "w2_scales": w2_scales,
        "shift": (0.6 * n(H) * u[:, 0]).astype(np.float32),
        "w3_words": w3_words, "w3_scales": w3_scales,
    }


def reference(tab_words, tab_scales, offs, pos1, pos2, pos3, pos4, w1, w2_words, w2_scales, shift, w3_words, w3_scales):
    v = unpack_weight(tab_words, tab_scales, "e4m3")[:, unstriped(offs)]
    w2 = unpack_weight(w2_words, w2_scales, "e2m1")
    w3 = unpack_weight(w3_words, w3_scales, "e4m3")
    claim = mxq(f64(w1), 0, "e4m3").T @ v
    doubt = w2.T @ v
    h = claim / (1.0 + np.abs(doubt))
    a1 = h[:, unstriped(pos1)] + h[:, unstriped(pos2)]
    precedent = h[:, unstriped(pos4)] + f64(shift)[:, None]
    a2 = np.maximum(a1[:, unstriped(pos3)], precedent)
    return w3.T @ mxq(a2, 0, "e4m3")

@@ -1,0 +1,235 @@
+from contextlib import ExitStack
+
+import concourse.mybir as mybir
+
+K, H, N, T, S, PAIRS, KEPT = 1024, 512, 512, 4096, 2048, 1024, 512
+FLOPS = 2 * (2 * K * H * S + H * N * KEPT)
+
+F32 = mybir.dt.float32
+BF16 = mybir.dt.bfloat16
+I32 = mybir.dt.int32
+U32 = mybir.dt.uint32
+U16 = mybir.dt.uint16
+U8 = mybir.dt.uint8
+FP8X4 = mybir.dt.float8_e4m3fn_x4
+FP4X4 = mybir.dt.float4_e2m1fn_x4
+ALU = mybir.AluOpType
+ACT = mybir.ActivationFunctionType
+
+P = 128
+PACK = 4
+PASSES = K // (P * PACK)
+CHUNK = 512
+CHUNKS = S // CHUNK
+HALF = KEPT // 2
+STRIPE = 16
+FREE_ROWS = P - K // 32
+
+
+def tile_list_intake_merit_scores_kernel(
+    tc, tab_words, tab_scales, offs, pos1, pos2, pos3, pos4, w1, w2_words, w2_scales, shift, w3_words, w3_scales, out
+):
+    nc = tc.nc
+    with ExitStack() as ctx:
+        keep = ctx.enter_context(tc.tile_pool(name="keep", bufs=1))
+        ring = ctx.enter_context(tc.tile_pool(name="ring", bufs=3))
+        psum = ctx.enter_context(tc.psum_pool(name="psum", bufs=4))
+
+        def held(name, shape, dtype):
+            return keep.tile(shape, dtype, name=name, align_bytes=64)
+
+        offs_sb = held("offs_sb", [P, S // STRIPE], U16)
+        pos1_sb = held("pos1_sb", [P, PAIRS // STRIPE], U16)
+        pos2_sb = held("pos2_sb", [P, PAIRS // STRIPE], U16)
+        pos3_sb = held("pos3_sb", [P, KEPT // STRIPE], U16)
+        pos4_sb = held("pos4_sb", [P, KEPT // STRIPE], U16)
+
+        tab_s = keep.tile([P, T], U8, name="tab_s", tag="early", align_bytes=64)
+        tab_w = [held("tab_w%d" % a, [P, T], U32) for a in range(PASSES)]
+        v_s = held("v_s", [P, S], U8)
+        v_planes = [held("v_plane%d" % a, [P, S], U8) for a in range(PASSES)]
+        w2_raw = keep.tile([P, PASSES, 2 * H], U8, name="w2_raw", tag="words", align_bytes=64)
+        w2s_raw = keep.tile([P, PASSES, H], U8, name="w2s_raw", tag="bytes8", align_bytes=64)
+        shift_sb = held("shift_sb", [P, PACK], F32)
+
+        nc.vector.memset(tab_s[:FREE_ROWS, :].bitcast(I32), 0)
+        nc.gpsimd.memset(w2s_raw[:].rearrange("p a c -> p (a c)").bitcast(I32), 0)
+        for a in range(PASSES):
+            nc.vector.memset(v_planes[a][:].bitcast(I32), 0)
+
+        def load_words(a):
+            nc.sync.dma_start(
+                out=tab_w[a][:].bitcast(I32), in_=tab_words[a].rearrange("p t i -> p (t i)").bitcast(I32)
+            )
+
+        nc.sync.dma_start(offs_sb[:], offs)
+        nc.sync.dma_start(
+            out=tab_s[FREE_ROWS:, :].bitcast(I32), in_=tab_scales.rearrange("a q t -> (a q) t").bitcast(I32)
+        )
+        load_words(0)
+        nc.sync.dma_start(out=w2_raw[:].bitcast(I32), in_=w2_words.rearrange("a p c -> p a c").bitcast(I32))
+        nc.sync.dma_start(pos1_sb[:], pos1)
+        nc.sync.dma_start(pos2_sb[:], pos2)
+        nc.sync.dma_start(pos3_sb[:], pos3)
+        nc.sync.dma_start(pos4_sb[:], pos4)
+        nc.sync.dma_start(out=shift_sb[:], in_=shift.rearrange("(p t) -> p t", t=PACK))
+        load_words(1)
+        for q in range(4):
+            nc.gpsimd.dma_start(
+                out=w2s_raw[32 * q : 32 * q + 4, :, :].bitcast(I32),
+                in_=w2_scales[:, 4 * q : 4 * q + 4, :].rearrange("a r c -> r a c").bitcast(I32),
+            )
+
+        nc.vector.tensor_copy(v_s[:], tab_s[:].indirect(offs_sb[:]))
+        for a in range(PASSES):
+            for q in range(4):
+                row = FREE_ROWS + 16 * a + 4 * q
+                nc.scalar.dma_start(
+                    out=v_planes[a][32 * q : 32 * q + 4, :].bitcast(I32), in_=v_s[row : row + 4, :].bitcast(I32)
+                )
+        w1_raw = keep.tile([P, PASSES, PACK, H], F32, name="w1_raw", tag="early", align_bytes=64)
+        for a in range(PASSES):
+            nc.sync.dma_start(
+                out=w1_raw[:, a], in_=w1[a * P * PACK : (a + 1) * P * PACK, :].rearrange("(p i) c -> p i c", i=PACK)
+            )
+
+        v_w = [[held("v_w%d_%d" % (a, c), [P, CHUNK], U32) for c in range(CHUNKS)] for a in range(PASSES)]
+
+        def gather_words(a):
+            cols = CHUNK // STRIPE
+            for c in range(CHUNKS):
+                nc.vector.tensor_copy(v_w[a][c][:], tab_w[a][:].indirect(offs_sb[:, c * cols : (c + 1) * cols]))
+
+        gather_words(0)
+
+        w2_w = held("w2_w", [P, PASSES, 2 * H], U8)
+        w2_s = held("w2_s", [P, PASSES, H], U8)
+        nc.vector.tensor_copy(
+            out=w2_w[:].bitcast(U16).rearrange("p a (t m) -> p a t m", t=PACK),
+            in_=w2_raw[:].bitcast(U16).rearrange("p a (m t) -> p a t m", t=PACK),
+        )
+        nc.vector.tensor_copy(
+            out=w2_s[:].rearrange("p a (t m) -> p a t m", t=PACK),
+            in_=w2s_raw[:].rearrange("p a (m t) -> p a t m", t=PACK),
+        )
+
+        w3_w = keep.tile([P, N], U32, name="w3_w", tag="words", align_bytes=64)
+        w3_s = keep.tile([P, N], U8, name="w3_s", tag="bytes8", align_bytes=64)
+        nc.gpsimd.memset(w3_s[:].bitcast(I32), 0)
+        nc.sync.dma_start(out=w3_w[:].bitcast(I32), in_=w3_words[0].rearrange("p c i -> p (c i)").bitcast(I32))
+        for q in range(4):
+            nc.sync.dma_start(
+                out=w3_s[32 * q : 32 * q + 4, :].bitcast(I32), in_=w3_scales[0, 4 * q : 4 * q + 4, :].bitcast(I32)
+            )
+
+        gather_words(1)
+
+        w1_w = [held("w1_w%d" % a, [P, H], U32) for a in range(PASSES)]
+        w1_s = [held("w1_s%d" % a, [P, H], U8) for a in range(PASSES)]
+        w1_bf = [held("w1_bf%d" % a, [P, H * PACK], BF16) for a in range(PASSES)]
+        for a in range(PASSES):
+            nc.vector.tensor_copy(
+                out=w1_bf[a][:].rearrange("p (t m i) -> p m t i", t=PACK, i=PACK),
+                in_=w1_raw[:, a].rearrange("p i (m t) -> p m t i", t=PACK),
+            )
+        for a in range(PASSES):
+            nc.vector.quantize_mx(out=w1_w[a][:].bitcast(FP8X4), scales=w1_s[a][:], in_=w1_bf[a][:])
+
+        h = [held("h%d" % t, [P, S], F32) for t in range(PACK)]
+        damp = [held("damp%d" % t, [P, S], F32) for t in range(PACK)]
+        a2 = held("a2", [P, PACK, KEPT], BF16)
+
+        def first_stage(t, c):
+            cols = slice(c * CHUNK, (c + 1) * CHUNK)
+            rows = slice(t * P, (t + 1) * P)
+            doubt = psum.tile([P, CHUNK], F32, name="doubt")
+            for a in range(PASSES):
+                nc.tensor.matmul_mx(
+                    out=doubt[:],
+                    lhsT=w2_w[:, a, 2 * t * P : 2 * (t + 1) * P].bitcast(FP4X4),
+                    lhsT_scale=w2_s[:, a, rows],
+                    rhs=v_w[a][c][:].bitcast(FP8X4),
+                    rhs_scale=v_planes[a][:, cols],
+                    start=(a == 0),
+                    stop=(a == PASSES - 1),
+                )
+            size = ring.tile([P, CHUNK], F32, name="size")
+            root = ring.tile([P, CHUNK], F32, name="root")
+            nc.scalar.activation(out=size[:], in_=doubt[:], func=ACT.Abs)
+            nc.scalar.activation(out=root[:], in_=size[:], func=ACT.Abs_reciprocal_sqrt, bias=1.0)
+            nc.scalar.activation(out=damp[t][:, cols], in_=root[:], func=ACT.Square)
+            claim = psum.tile([P, CHUNK], F32, name="claim")
+            for a in range(PASSES):
+                nc.tensor.matmul_mx(
+                    out=claim[:],
+                    lhsT=w1_w[a][:, rows].bitcast(FP8X4),
+                    lhsT_scale=w1_s[a][:, rows],
+                    rhs=v_w[a][c][:].bitcast(FP8X4),
+                    rhs_scale=v_planes[a][:, cols],
+                    start=(a == 0),
+                    stop=(a == PASSES - 1),
+                )
+            nc.vector.tensor_tensor(out=h[t][:, cols], in0=claim[:], in1=damp[t][:, cols], op=ALU.mult)
+
+        def pairs(t):
+            first = ring.tile([P, PAIRS], F32, name="first")
+            a1 = ring.tile([P, PAIRS], F32, name="a1")
+            nc.vector.tensor_copy(first[:], h[t][:].indirect(pos1_sb[:]))
+            nc.vector.tensor_tensor(a1[:], h[t][:].indirect(pos2_sb[:]), first[:], ALU.add)
+            return a1
+
+        def kept(t, a1, j0, width):
+            lst = slice(j0 // STRIPE, (j0 + width) // STRIPE)
+            precedent = ring.tile([P, width], F32, name="precedent")
+            pair = ring.tile([P, width], F32, name="pair")
+            nc.vector.tensor_copy(precedent[:], h[t][:].indirect(pos4_sb[:, lst]))
+            nc.vector.tensor_copy(pair[:], a1[:].indirect(pos3_sb[:, lst]))
+            nc.vector.scalar_tensor_tensor(
+                out=a2[:, t, j0 : j0 + width],
+                in0=precedent[:],
+                scalar=shift_sb[:, t : t + 1],
+                in1=pair[:],
+                op0=ALU.add,
+                op1=ALU.max,
+            )
+
+        def last_stage(j0, weave):
+            woven = ring.tile([P, HALF * PACK], BF16, name="woven", align_bytes=64)
+            a2_w = ring.tile([P, HALF], U32, name="a2_w", align_bytes=64)
+            a2_s = ring.tile([P, HALF], U8, name="a2_s", align_bytes=64)
+            weave(
+                out=woven[:].rearrange("p (c i t) -> p c t i", i=4, t=PACK),
+                in_=a2[:, :, j0 : j0 + HALF].rearrange("p t (c i) -> p c t i", i=4),
+            )
+            nc.vector.quantize_mx(out=a2_w[:].bitcast(FP8X4), scales=a2_s[:], in_=woven[:])
+            for b, evacuate in enumerate((nc.scalar.copy, nc.vector.tensor_copy if j0 else nc.scalar.copy)):
+                acc = psum.tile([P, 2, HALF], F32, name="doubt")
+                for g in range(2):
+                    rows = slice((2 * b + g) * P, (2 * b + g + 1) * P)
+                    nc.tensor.matmul_mx(
+                        out=acc[:, g, :],
+                        lhsT=w3_w[:, rows].bitcast(FP8X4),
+                        lhsT_scale=w3_s[:, rows],
+                        rhs=a2_w[:].bitcast(FP8X4),
+                        rhs_scale=a2_s[:],
+                        start=True,
+                        stop=True,
+                    )
+                result = keep.tile([P, 2, HALF], F32, name="result%d_%d" % (j0, b))
+                evacuate(out=result[:], in_=acc[:])
+                nc.sync.dma_start(
+                    out=out[2 * b * P : 2 * (b + 1) * P, j0 : j0 + HALF].rearrange("(g p) j -> p g j", g=2),
+                    in_=result[:],
+                )
+
+        for t in range(PACK):
+            for c in range(CHUNKS):
+                first_stage(t, c)
+            a1 = pairs(t)
+            if t < PACK - 1:
+                kept(t, a1, 0, KEPT)
+            else:
+                kept(t, a1, 0, HALF)
+                kept(t, a1, HALF, HALF)
+        last_stage(0, nc.scalar.copy)
+        last_stage(HALF, nc.vector.tensor_copy)

@@ -46,21 +46,29 @@ def tile_list_intake_merit_scores_kernel(
 
         tab_s = keep.tile([P, T], U8, name="tab_s", tag="early", align_bytes=64)
         tab_w = [held("tab_w%d" % a, [P, T], U32) for a in range(PASSES)]
+        w1_raw = [keep.tile([P, PACK, H], F32, name="w1_raw0", tag="first", align_bytes=64)]
         v_s = held("v_s", [P, S], U8)
         v_planes = [held("v_plane%d" % a, [P, S], U8) for a in range(PASSES)]
         w2_raw = keep.tile([P, PASSES, 2 * H], U8, name="w2_raw", tag="words", align_bytes=64)
         w2s_raw = keep.tile([P, PASSES, H], U8, name="w2s_raw", tag="bytes8", align_bytes=64)
-        shift_sb = held("shift_sb", [P, PACK], F32)
 
         nc.vector.memset(tab_s[:FREE_ROWS, :].bitcast(I32), 0)
         nc.gpsimd.memset(w2s_raw[:].rearrange("p a c -> p (a c)").bitcast(I32), 0)
         for a in range(PASSES):
             nc.vector.memset(v_planes[a][:].bitcast(I32), 0)
 
+        warm = held("warm", [P, 2], F32)
+        nc.vector.memset(warm[:, 0:1], 1.0)
+        nc.scalar.activation(out=warm[:, 1:2], in_=warm[:, 0:1], func=ACT.Abs_reciprocal_sqrt, bias=1.0)
+
         def load_words(a):
             nc.sync.dma_start(
                 out=tab_w[a][:].bitcast(I32), in_=tab_words[a].rearrange("p t i -> p (t i)").bitcast(I32)
             )
+
+        def load_w1(a):
+            rows = w1[a * P * PACK : (a + 1) * P * PACK, :]
+            nc.sync.dma_start(out=w1_raw[a][:], in_=rows.rearrange("(p i) c -> p i c", i=PACK))
 
         nc.sync.dma_start(offs_sb[:], offs)
         nc.sync.dma_start(
@@ -70,10 +78,10 @@ def tile_list_intake_merit_scores_kernel(
         nc.sync.dma_start(out=w2_raw[:].bitcast(I32), in_=w2_words.rearrange("a p c -> p a c").bitcast(I32))
         nc.sync.dma_start(pos1_sb[:], pos1)
         nc.sync.dma_start(pos2_sb[:], pos2)
+        load_w1(0)
         nc.sync.dma_start(pos3_sb[:], pos3)
-        nc.sync.dma_start(pos4_sb[:], pos4)
-        nc.sync.dma_start(out=shift_sb[:], in_=shift.rearrange("(p t) -> p t", t=PACK))
         load_words(1)
+        nc.sync.dma_start(pos4_sb[:], pos4)
         for q in range(4):
             nc.gpsimd.dma_start(
                 out=w2s_raw[32 * q : 32 * q + 4, :, :].bitcast(I32),
@@ -84,23 +92,13 @@ def tile_list_intake_merit_scores_kernel(
         for a in range(PASSES):
             for q in range(4):
                 row = FREE_ROWS + 16 * a + 4 * q
-                nc.scalar.dma_start(
+                queue = (nc.scalar, nc.gpsimd)[a]
+                queue.dma_start(
                     out=v_planes[a][32 * q : 32 * q + 4, :].bitcast(I32), in_=v_s[row : row + 4, :].bitcast(I32)
                 )
-        w1_raw = keep.tile([P, PASSES, PACK, H], F32, name="w1_raw", tag="early", align_bytes=64)
-        for a in range(PASSES):
-            nc.sync.dma_start(
-                out=w1_raw[:, a], in_=w1[a * P * PACK : (a + 1) * P * PACK, :].rearrange("(p i) c -> p i c", i=PACK)
-            )
 
-        v_w = [[held("v_w%d_%d" % (a, c), [P, CHUNK], U32) for c in range(CHUNKS)] for a in range(PASSES)]
-
-        def gather_words(a):
-            cols = CHUNK // STRIPE
-            for c in range(CHUNKS):
-                nc.vector.tensor_copy(v_w[a][c][:], tab_w[a][:].indirect(offs_sb[:, c * cols : (c + 1) * cols]))
-
-        gather_words(0)
+        w1_raw.append(keep.tile([P, PACK, H], F32, name="w1_raw1", tag="early", align_bytes=64))
+        load_w1(1)
 
         w2_w = held("w2_w", [P, PASSES, 2 * H], U8)
         w2_s = held("w2_s", [P, PASSES, H], U8)
@@ -113,123 +111,147 @@ def tile_list_intake_merit_scores_kernel(
             in_=w2s_raw[:].rearrange("p a (m t) -> p a t m", t=PACK),
         )
 
-        w3_w = keep.tile([P, N], U32, name="w3_w", tag="words", align_bytes=64)
+        shift_sb = keep.tile([P, PACK], F32, name="shift_sb", tag="words", align_bytes=64)
+        nc.sync.dma_start(out=shift_sb[:], in_=shift.rearrange("(p t) -> p t", t=PACK))
+
+        v_w0 = held("v_w0", [P, S], U32)
+        nc.vector.tensor_copy(v_w0[:], tab_w[0][:].indirect(offs_sb[:]))
+        v_w = [[v_w0[:, c * CHUNK : (c + 1) * CHUNK] for c in range(CHUNKS)]]
+
+        w1_w = [held("w1_w%d" % a, [P, H], U32) for a in range(PASSES)]
+        w1_s = [held("w1_s%d" % a, [P, H], U8) for a in range(PASSES)]
+        w1_bf = [held("w1_bf%d" % a, [P, H * PACK], BF16) for a in range(PASSES)]
+
+        def round_w1(a, copy):
+            copy(
+                out=w1_bf[a][:].rearrange("p (t m i) -> p m t i", t=PACK, i=PACK),
+                in_=w1_raw[a][:].rearrange("p i (m t) -> p m t i", t=PACK),
+            )
+
+        def quantise_w1(a):
+            nc.vector.quantize_mx(out=w1_w[a][:].bitcast(FP8X4), scales=w1_s[a][:], in_=w1_bf[a][:])
+
+        round_w1(0, nc.scalar.copy)
+        quantise_w1(0)
+
+        w3_w = keep.tile([P, N], U32, name="w3_w", tag="first", align_bytes=64)
         w3_s = keep.tile([P, N], U8, name="w3_s", tag="bytes8", align_bytes=64)
-        nc.gpsimd.memset(w3_s[:].bitcast(I32), 0)
+        nc.vector.memset(w3_s[:].bitcast(I32), 0)
         nc.sync.dma_start(out=w3_w[:].bitcast(I32), in_=w3_words[0].rearrange("p c i -> p (c i)").bitcast(I32))
         for q in range(4):
             nc.sync.dma_start(
                 out=w3_s[32 * q : 32 * q + 4, :].bitcast(I32), in_=w3_scales[0, 4 * q : 4 * q + 4, :].bitcast(I32)
             )
 
-        gather_words(1)
+        v_w1 = [held("v_w1_%d" % c, [P, CHUNK], U32) for c in range(CHUNKS)]
+        for c in range(CHUNKS):
+            cols = slice(c * CHUNK // STRIPE, (c + 1) * CHUNK // STRIPE)
+            nc.vector.tensor_copy(v_w1[c][:], tab_w[1][:].indirect(offs_sb[:, cols]))
+        v_w.append([v_w1[c][:] for c in range(CHUNKS)])
 
-        w1_w = [held("w1_w%d" % a, [P, H], U32) for a in range(PASSES)]
-        w1_s = [held("w1_s%d" % a, [P, H], U8) for a in range(PASSES)]
-        w1_bf = [held("w1_bf%d" % a, [P, H * PACK], BF16) for a in range(PASSES)]
-        for a in range(PASSES):
-            nc.vector.tensor_copy(
-                out=w1_bf[a][:].rearrange("p (t m i) -> p m t i", t=PACK, i=PACK),
-                in_=w1_raw[:, a].rearrange("p i (m t) -> p m t i", t=PACK),
-            )
-        for a in range(PASSES):
-            nc.vector.quantize_mx(out=w1_w[a][:].bitcast(FP8X4), scales=w1_s[a][:], in_=w1_bf[a][:])
+        round_w1(1, nc.vector.tensor_copy)
+        quantise_w1(1)
 
         h = [held("h%d" % t, [P, S], F32) for t in range(PACK)]
         damp = [held("damp%d" % t, [P, S], F32) for t in range(PACK)]
-        a2 = held("a2", [P, PACK, KEPT], BF16)
+        pair = held("pair", [P, PACK, KEPT], F32)
+        precedent = held("precedent", [P, PACK, KEPT], F32)
 
-        def first_stage(t, c):
+        steps = [(t, c) for t in range(PACK) for c in range(CHUNKS)]
+        sizes = {}
+        roots = {}
+
+        def product(name, words, scales, fmt, c):
+            acc = psum.tile([P, CHUNK], F32, name=name)
+            for a in range(PASSES):
+                nc.tensor.matmul_mx(
+                    out=acc[:],
+                    lhsT=words[a].bitcast(fmt),
+                    lhsT_scale=scales[a],
+                    rhs=v_w[a][c].bitcast(FP8X4),
+                    rhs_scale=v_planes[a][:, c * CHUNK : (c + 1) * CHUNK],
+                    start=(a == 0),
+                    stop=(a == PASSES - 1),
+                )
+            return acc
+
+        def doubt_size(step):
+            t, c = step
+            words = [w2_w[:, a, 2 * t * P : 2 * (t + 1) * P] for a in range(PASSES)]
+            scales = [w2_s[:, a, t * P : (t + 1) * P] for a in range(PASSES)]
+            doubt = product("doubt", words, scales, FP4X4, c)
+            sizes[step] = ring.tile([P, CHUNK], F32, name="size")
+            nc.scalar.activation(out=sizes[step][:], in_=doubt[:], func=ACT.Abs)
+
+        def doubt_root(step):
+            roots[step] = ring.tile([P, CHUNK], F32, name="root")
+            nc.scalar.activation(out=roots[step][:], in_=sizes[step][:], func=ACT.Abs_reciprocal_sqrt, bias=1.0)
+
+        def temper(step):
+            t, c = step
             cols = slice(c * CHUNK, (c + 1) * CHUNK)
-            rows = slice(t * P, (t + 1) * P)
-            doubt = psum.tile([P, CHUNK], F32, name="doubt")
-            for a in range(PASSES):
-                nc.tensor.matmul_mx(
-                    out=doubt[:],
-                    lhsT=w2_w[:, a, 2 * t * P : 2 * (t + 1) * P].bitcast(FP4X4),
-                    lhsT_scale=w2_s[:, a, rows],
-                    rhs=v_w[a][c][:].bitcast(FP8X4),
-                    rhs_scale=v_planes[a][:, cols],
-                    start=(a == 0),
-                    stop=(a == PASSES - 1),
-                )
-            size = ring.tile([P, CHUNK], F32, name="size")
-            root = ring.tile([P, CHUNK], F32, name="root")
-            nc.scalar.activation(out=size[:], in_=doubt[:], func=ACT.Abs)
-            nc.scalar.activation(out=root[:], in_=size[:], func=ACT.Abs_reciprocal_sqrt, bias=1.0)
-            nc.scalar.activation(out=damp[t][:, cols], in_=root[:], func=ACT.Square)
-            claim = psum.tile([P, CHUNK], F32, name="claim")
-            for a in range(PASSES):
-                nc.tensor.matmul_mx(
-                    out=claim[:],
-                    lhsT=w1_w[a][:, rows].bitcast(FP8X4),
-                    lhsT_scale=w1_s[a][:, rows],
-                    rhs=v_w[a][c][:].bitcast(FP8X4),
-                    rhs_scale=v_planes[a][:, cols],
-                    start=(a == 0),
-                    stop=(a == PASSES - 1),
-                )
+            nc.scalar.activation(out=damp[t][:, cols], in_=roots[step][:], func=ACT.Square)
+            words = [w1_w[a][:, t * P : (t + 1) * P] for a in range(PASSES)]
+            scales = [w1_s[a][:, t * P : (t + 1) * P] for a in range(PASSES)]
+            claim = product("claim", words, scales, FP8X4, c)
             nc.vector.tensor_tensor(out=h[t][:, cols], in0=claim[:], in1=damp[t][:, cols], op=ALU.mult)
 
-        def pairs(t):
+        def pick_pairs(t):
             first = ring.tile([P, PAIRS], F32, name="first")
+            picked = ring.tile([P, KEPT], F32, name="picked")
             a1 = ring.tile([P, PAIRS], F32, name="a1")
             nc.vector.tensor_copy(first[:], h[t][:].indirect(pos1_sb[:]))
+            nc.vector.tensor_copy(picked[:], h[t][:].indirect(pos4_sb[:]))
             nc.vector.tensor_tensor(a1[:], h[t][:].indirect(pos2_sb[:]), first[:], ALU.add)
+            nc.scalar.activation(
+                out=precedent[:, t, :], in_=picked[:], func=ACT.Identity, bias=shift_sb[:, t : t + 1]
+            )
             return a1
 
-        def kept(t, a1, j0, width):
-            lst = slice(j0 // STRIPE, (j0 + width) // STRIPE)
-            precedent = ring.tile([P, width], F32, name="precedent")
-            pair = ring.tile([P, width], F32, name="pair")
-            nc.vector.tensor_copy(precedent[:], h[t][:].indirect(pos4_sb[:, lst]))
-            nc.vector.tensor_copy(pair[:], a1[:].indirect(pos3_sb[:, lst]))
-            nc.vector.scalar_tensor_tensor(
-                out=a2[:, t, j0 : j0 + width],
-                in0=precedent[:],
-                scalar=shift_sb[:, t : t + 1],
-                in1=pair[:],
-                op0=ALU.add,
-                op1=ALU.max,
-            )
+        def pick_kept(t, a1, j0, width):
+            entries = slice(j0 // STRIPE, (j0 + width) // STRIPE)
+            nc.vector.tensor_copy(pair[:, t, j0 : j0 + width], a1[:].indirect(pos3_sb[:, entries]))
 
-        def last_stage(j0, weave):
-            woven = ring.tile([P, HALF * PACK], BF16, name="woven", align_bytes=64)
+        def last_stage(j0, bank, evacuate):
+            cols = slice(j0, j0 + HALF)
+            a2 = ring.tile([P, HALF * PACK], BF16, name="a2", align_bytes=64)
             a2_w = ring.tile([P, HALF], U32, name="a2_w", align_bytes=64)
             a2_s = ring.tile([P, HALF], U8, name="a2_s", align_bytes=64)
-            weave(
-                out=woven[:].rearrange("p (c i t) -> p c t i", i=4, t=PACK),
-                in_=a2[:, :, j0 : j0 + HALF].rearrange("p t (c i) -> p c t i", i=4),
+            nc.vector.tensor_tensor(
+                out=a2[:].rearrange("p (c i t) -> p c t i", i=4, t=PACK),
+                in0=pair[:, :, cols].rearrange("p t (c i) -> p c t i", i=4),
+                in1=precedent[:, :, cols].rearrange("p t (c i) -> p c t i", i=4),
+                op=ALU.max,
             )
-            nc.vector.quantize_mx(out=a2_w[:].bitcast(FP8X4), scales=a2_s[:], in_=woven[:])
-            for b, evacuate in enumerate((nc.scalar.copy, nc.vector.tensor_copy if j0 else nc.scalar.copy)):
-                acc = psum.tile([P, 2, HALF], F32, name="doubt")
-                for g in range(2):
-                    rows = slice((2 * b + g) * P, (2 * b + g + 1) * P)
-                    nc.tensor.matmul_mx(
-                        out=acc[:, g, :],
-                        lhsT=w3_w[:, rows].bitcast(FP8X4),
-                        lhsT_scale=w3_s[:, rows],
-                        rhs=a2_w[:].bitcast(FP8X4),
-                        rhs_scale=a2_s[:],
-                        start=True,
-                        stop=True,
-                    )
-                result = keep.tile([P, 2, HALF], F32, name="result%d_%d" % (j0, b))
-                evacuate(out=result[:], in_=acc[:])
-                nc.sync.dma_start(
-                    out=out[2 * b * P : 2 * (b + 1) * P, j0 : j0 + HALF].rearrange("(g p) j -> p g j", g=2),
-                    in_=result[:],
+            nc.vector.quantize_mx(out=a2_w[:].bitcast(FP8X4), scales=a2_s[:], in_=a2[:])
+            for g in range(N // P):
+                rows = slice(g * P, (g + 1) * P)
+                acc = psum.tile([P, HALF], F32, name=bank)
+                nc.tensor.matmul_mx(
+                    out=acc[:],
+                    lhsT=w3_w[:, rows].bitcast(FP8X4),
+                    lhsT_scale=w3_s[:, rows],
+                    rhs=a2_w[:].bitcast(FP8X4),
+                    rhs_scale=a2_s[:],
+                    start=True,
+                    stop=True,
                 )
+                result = keep.tile([P, HALF], F32, name="result%d_%d" % (j0, g))
+                evacuate[g % 2](out=result[:], in_=acc[:])
+                nc.sync.dma_start(out=out[rows, cols], in_=result[:])
 
-        for t in range(PACK):
-            for c in range(CHUNKS):
-                first_stage(t, c)
-            a1 = pairs(t)
-            if t < PACK - 1:
-                kept(t, a1, 0, KEPT)
-            else:
-                kept(t, a1, 0, HALF)
-                kept(t, a1, HALF, HALF)
-        last_stage(0, nc.scalar.copy)
-        last_stage(HALF, nc.vector.tensor_copy)
+        doubt_size(steps[0])
+        for n, step in enumerate(steps):
+            doubt_root(step)
+            if n + 1 < len(steps):
+                doubt_size(steps[n + 1])
+            temper(step)
+            t, c = step
+            if c == CHUNKS - 1:
+                a1 = pick_pairs(t)
+                if t < PACK - 1:
+                    pick_kept(t, a1, 0, KEPT)
+        pick_kept(PACK - 1, a1, 0, HALF)
+        pick_kept(PACK - 1, a1, HALF, HALF)
+        last_stage(0, "doubt", (nc.scalar.copy, nc.scalar.copy))
+        last_stage(HALF, "claim", (nc.scalar.copy, nc.vector.tensor_copy))

from contextlib import ExitStack

import concourse.mybir as mybir

K, H, N, T, S, PAIRS, KEPT = 1024, 512, 512, 4096, 2048, 1024, 512
FLOPS = 2 * (2 * K * H * S + H * N * KEPT)

F32 = mybir.dt.float32
BF16 = mybir.dt.bfloat16
I32 = mybir.dt.int32
U32 = mybir.dt.uint32
U16 = mybir.dt.uint16
U8 = mybir.dt.uint8
FP8X4 = mybir.dt.float8_e4m3fn_x4
FP4X4 = mybir.dt.float4_e2m1fn_x4
ALU = mybir.AluOpType
ACT = mybir.ActivationFunctionType

P = 128
PACK = 4
PASSES = K // (P * PACK)
CHUNK = 512
CHUNKS = S // CHUNK
HALF = KEPT // 2
STRIPE = 16
FREE_ROWS = P - K // 32


def tile_list_intake_merit_scores_kernel(
    tc, tab_words, tab_scales, offs, pos1, pos2, pos3, pos4, w1, w2_words, w2_scales, shift, w3_words, w3_scales, out
):
    nc = tc.nc
    with ExitStack() as ctx:
        keep = ctx.enter_context(tc.tile_pool(name="keep", bufs=1))
        ring = ctx.enter_context(tc.tile_pool(name="ring", bufs=3))
        psum = ctx.enter_context(tc.psum_pool(name="psum", bufs=4))

        def held(name, shape, dtype):
            return keep.tile(shape, dtype, name=name, align_bytes=64)

        offs_sb = held("offs_sb", [P, S // STRIPE], U16)
        pos1_sb = held("pos1_sb", [P, PAIRS // STRIPE], U16)
        pos2_sb = held("pos2_sb", [P, PAIRS // STRIPE], U16)
        pos3_sb = held("pos3_sb", [P, KEPT // STRIPE], U16)
        pos4_sb = held("pos4_sb", [P, KEPT // STRIPE], U16)

        tab_s = keep.tile([P, T], U8, name="tab_s", tag="early", align_bytes=64)
        tab_w = [held("tab_w%d" % a, [P, T], U32) for a in range(PASSES)]
        w1_raw = [keep.tile([P, PACK, H], F32, name="w1_raw0", tag="first", align_bytes=64)]
        v_s = held("v_s", [P, S], U8)
        v_planes = [held("v_plane%d" % a, [P, S], U8) for a in range(PASSES)]
        w2_raw = keep.tile([P, PASSES, 2 * H], U8, name="w2_raw", tag="words", align_bytes=64)
        w2s_raw = keep.tile([P, PASSES, H], U8, name="w2s_raw", tag="bytes8", align_bytes=64)

        nc.vector.memset(tab_s[:FREE_ROWS, :].bitcast(I32), 0)
        nc.gpsimd.memset(w2s_raw[:].rearrange("p a c -> p (a c)").bitcast(I32), 0)
        for a in range(PASSES):
            nc.vector.memset(v_planes[a][:].bitcast(I32), 0)

        warm = held("warm", [P, 2], F32)
        nc.vector.memset(warm[:, 0:1], 1.0)
        nc.scalar.activation(out=warm[:, 1:2], in_=warm[:, 0:1], func=ACT.Abs_reciprocal_sqrt, bias=1.0)

        def load_words(a):
            nc.sync.dma_start(
                out=tab_w[a][:].bitcast(I32), in_=tab_words[a].rearrange("p t i -> p (t i)").bitcast(I32)
            )

        def load_w1(a):
            rows = w1[a * P * PACK : (a + 1) * P * PACK, :]
            nc.sync.dma_start(out=w1_raw[a][:], in_=rows.rearrange("(p i) c -> p i c", i=PACK))

        nc.sync.dma_start(offs_sb[:], offs)
        nc.sync.dma_start(
            out=tab_s[FREE_ROWS:, :].bitcast(I32), in_=tab_scales.rearrange("a q t -> (a q) t").bitcast(I32)
        )
        load_words(0)
        nc.sync.dma_start(out=w2_raw[:].bitcast(I32), in_=w2_words.rearrange("a p c -> p a c").bitcast(I32))
        nc.sync.dma_start(pos1_sb[:], pos1)
        nc.sync.dma_start(pos2_sb[:], pos2)
        load_w1(0)
        nc.sync.dma_start(pos3_sb[:], pos3)
        load_words(1)
        nc.sync.dma_start(pos4_sb[:], pos4)
        for q in range(4):
            nc.gpsimd.dma_start(
                out=w2s_raw[32 * q : 32 * q + 4, :, :].bitcast(I32),
                in_=w2_scales[:, 4 * q : 4 * q + 4, :].rearrange("a r c -> r a c").bitcast(I32),
            )

        nc.vector.tensor_copy(v_s[:], tab_s[:].indirect(offs_sb[:]))
        for a in range(PASSES):
            for q in range(4):
                row = FREE_ROWS + 16 * a + 4 * q
                queue = (nc.scalar, nc.gpsimd)[a]
                queue.dma_start(
                    out=v_planes[a][32 * q : 32 * q + 4, :].bitcast(I32), in_=v_s[row : row + 4, :].bitcast(I32)
                )

        w1_raw.append(keep.tile([P, PACK, H], F32, name="w1_raw1", tag="early", align_bytes=64))
        load_w1(1)

        w2_w = held("w2_w", [P, PASSES, 2 * H], U8)
        w2_s = held("w2_s", [P, PASSES, H], U8)
        nc.vector.tensor_copy(
            out=w2_w[:].bitcast(U16).rearrange("p a (t m) -> p a t m", t=PACK),
            in_=w2_raw[:].bitcast(U16).rearrange("p a (m t) -> p a t m", t=PACK),
        )
        nc.vector.tensor_copy(
            out=w2_s[:].rearrange("p a (t m) -> p a t m", t=PACK),
            in_=w2s_raw[:].rearrange("p a (m t) -> p a t m", t=PACK),
        )

        shift_sb = keep.tile([P, PACK], F32, name="shift_sb", tag="words", align_bytes=64)
        nc.sync.dma_start(out=shift_sb[:], in_=shift.rearrange("(p t) -> p t", t=PACK))

        v_w0 = held("v_w0", [P, S], U32)
        nc.vector.tensor_copy(v_w0[:], tab_w[0][:].indirect(offs_sb[:]))
        v_w = [[v_w0[:, c * CHUNK : (c + 1) * CHUNK] for c in range(CHUNKS)]]

        w1_w = [held("w1_w%d" % a, [P, H], U32) for a in range(PASSES)]
        w1_s = [held("w1_s%d" % a, [P, H], U8) for a in range(PASSES)]
        w1_bf = [held("w1_bf%d" % a, [P, H * PACK], BF16) for a in range(PASSES)]

        def round_w1(a, copy):
            copy(
                out=w1_bf[a][:].rearrange("p (t m i) -> p m t i", t=PACK, i=PACK),
                in_=w1_raw[a][:].rearrange("p i (m t) -> p m t i", t=PACK),
            )

        def quantise_w1(a):
            nc.vector.quantize_mx(out=w1_w[a][:].bitcast(FP8X4), scales=w1_s[a][:], in_=w1_bf[a][:])

        round_w1(0, nc.scalar.copy)
        quantise_w1(0)

        w3_w = keep.tile([P, N], U32, name="w3_w", tag="first", align_bytes=64)
        w3_s = keep.tile([P, N], U8, name="w3_s", tag="bytes8", align_bytes=64)
        nc.vector.memset(w3_s[:].bitcast(I32), 0)
        nc.sync.dma_start(out=w3_w[:].bitcast(I32), in_=w3_words[0].rearrange("p c i -> p (c i)").bitcast(I32))
        for q in range(4):
            nc.sync.dma_start(
                out=w3_s[32 * q : 32 * q + 4, :].bitcast(I32), in_=w3_scales[0, 4 * q : 4 * q + 4, :].bitcast(I32)
            )

        v_w1 = [held("v_w1_%d" % c, [P, CHUNK], U32) for c in range(CHUNKS)]
        for c in range(CHUNKS):
            cols = slice(c * CHUNK // STRIPE, (c + 1) * CHUNK // STRIPE)
            nc.vector.tensor_copy(v_w1[c][:], tab_w[1][:].indirect(offs_sb[:, cols]))
        v_w.append([v_w1[c][:] for c in range(CHUNKS)])

        round_w1(1, nc.vector.tensor_copy)
        quantise_w1(1)

        h = [held("h%d" % t, [P, S], F32) for t in range(PACK)]
        damp = [held("damp%d" % t, [P, S], F32) for t in range(PACK)]
        pair = held("pair", [P, PACK, KEPT], F32)
        precedent = held("precedent", [P, PACK, KEPT], F32)

        steps = [(t, c) for t in range(PACK) for c in range(CHUNKS)]
        sizes = {}
        roots = {}

        def product(name, words, scales, fmt, c):
            acc = psum.tile([P, CHUNK], F32, name=name)
            for a in range(PASSES):
                nc.tensor.matmul_mx(
                    out=acc[:],
                    lhsT=words[a].bitcast(fmt),
                    lhsT_scale=scales[a],
                    rhs=v_w[a][c].bitcast(FP8X4),
                    rhs_scale=v_planes[a][:, c * CHUNK : (c + 1) * CHUNK],
                    start=(a == 0),
                    stop=(a == PASSES - 1),
                )
            return acc

        def doubt_size(step):
            t, c = step
            words = [w2_w[:, a, 2 * t * P : 2 * (t + 1) * P] for a in range(PASSES)]
            scales = [w2_s[:, a, t * P : (t + 1) * P] for a in range(PASSES)]
            doubt = product("doubt", words, scales, FP4X4, c)
            sizes[step] = ring.tile([P, CHUNK], F32, name="size")
            nc.scalar.activation(out=sizes[step][:], in_=doubt[:], func=ACT.Abs)

        def doubt_root(step):
            roots[step] = ring.tile([P, CHUNK], F32, name="root")
            nc.scalar.activation(out=roots[step][:], in_=sizes[step][:], func=ACT.Abs_reciprocal_sqrt, bias=1.0)

        def temper(step):
            t, c = step
            cols = slice(c * CHUNK, (c + 1) * CHUNK)
            nc.scalar.activation(out=damp[t][:, cols], in_=roots[step][:], func=ACT.Square)
            words = [w1_w[a][:, t * P : (t + 1) * P] for a in range(PASSES)]
            scales = [w1_s[a][:, t * P : (t + 1) * P] for a in range(PASSES)]
            claim = product("claim", words, scales, FP8X4, c)
            nc.vector.tensor_tensor(out=h[t][:, cols], in0=claim[:], in1=damp[t][:, cols], op=ALU.mult)

        def pick_pairs(t):
            first = ring.tile([P, PAIRS], F32, name="first")
            picked = ring.tile([P, KEPT], F32, name="picked")
            a1 = ring.tile([P, PAIRS], F32, name="a1")
            nc.vector.tensor_copy(first[:], h[t][:].indirect(pos1_sb[:]))
            nc.vector.tensor_copy(picked[:], h[t][:].indirect(pos4_sb[:]))
            nc.vector.tensor_tensor(a1[:], h[t][:].indirect(pos2_sb[:]), first[:], ALU.add)
            nc.scalar.activation(
                out=precedent[:, t, :], in_=picked[:], func=ACT.Identity, bias=shift_sb[:, t : t + 1]
            )
            return a1

        def pick_kept(t, a1, j0, width):
            entries = slice(j0 // STRIPE, (j0 + width) // STRIPE)
            nc.vector.tensor_copy(pair[:, t, j0 : j0 + width], a1[:].indirect(pos3_sb[:, entries]))

        def last_stage(j0, bank, evacuate):
            cols = slice(j0, j0 + HALF)
            a2 = ring.tile([P, HALF * PACK], BF16, name="a2", align_bytes=64)
            a2_w = ring.tile([P, HALF], U32, name="a2_w", align_bytes=64)
            a2_s = ring.tile([P, HALF], U8, name="a2_s", align_bytes=64)
            nc.vector.tensor_tensor(
                out=a2[:].rearrange("p (c i t) -> p c t i", i=4, t=PACK),
                in0=pair[:, :, cols].rearrange("p t (c i) -> p c t i", i=4),
                in1=precedent[:, :, cols].rearrange("p t (c i) -> p c t i", i=4),
                op=ALU.max,
            )
            nc.vector.quantize_mx(out=a2_w[:].bitcast(FP8X4), scales=a2_s[:], in_=a2[:])
            for g in range(N // P):
                rows = slice(g * P, (g + 1) * P)
                acc = psum.tile([P, HALF], F32, name=bank)
                nc.tensor.matmul_mx(
                    out=acc[:],
                    lhsT=w3_w[:, rows].bitcast(FP8X4),
                    lhsT_scale=w3_s[:, rows],
                    rhs=a2_w[:].bitcast(FP8X4),
                    rhs_scale=a2_s[:],
                    start=True,
                    stop=True,
                )
                result = keep.tile([P, HALF], F32, name="result%d_%d" % (j0, g))
                evacuate[g % 2](out=result[:], in_=acc[:])
                nc.sync.dma_start(out=out[rows, cols], in_=result[:])

        doubt_size(steps[0])
        for n, step in enumerate(steps):
            doubt_root(step)
            if n + 1 < len(steps):
                doubt_size(steps[n + 1])
            temper(step)
            t, c = step
            if c == CHUNKS - 1:
                a1 = pick_pairs(t)
                if t < PACK - 1:
                    pick_kept(t, a1, 0, KEPT)
        pick_kept(PACK - 1, a1, 0, HALF)
        pick_kept(PACK - 1, a1, HALF, HALF)
        last_stage(0, "doubt", (nc.scalar.copy, nc.scalar.copy))
        last_stage(HALF, "claim", (nc.scalar.copy, nc.vector.tensor_copy))
